import numpy as np, ml_dtypes
CORES = [73,201,329,457,330]
N = 5
F = 256
def setup_inputs(rng):
    return {"x": rng.standard_normal((N, 128, N * F), dtype=np.float32).astype(ml_dtypes.bfloat16), "w": rng.standard_normal((N, 128, 128), dtype=np.float32).astype(ml_dtypes.bfloat16)}
def setup_inputs_big(rng):
    d = setup_inputs(rng)
    for k in ("x", "w"): d[k] = (d[k].astype(np.float32) * 1024.0).astype(d[k].dtype)
    return d
def setup_inputs_small(rng):
    d = setup_inputs(rng)
    for k in ("x", "w"): d[k] = (d[k].astype(np.float32) * (1 / 1024.0)).astype(d[k].dtype)
    return d
def setup_inputs_apart(rng):
    d = setup_inputs(rng)
    f = (10.0 ** rng.permutation(np.linspace(-1.5, 1.5, N))).astype(np.float32).reshape(N, 1, 1)
    for k in ("x", "w"): d[k] = (d[k].astype(np.float32) * f).astype(d[k].dtype)
    return d
def reference(x, w):
    X, W = x.astype(np.float64), w.astype(np.float64)
    s = X.sum(axis=0)
    o = np.concatenate([W[r].T @ s[:, F * r:F * r + F] for r in range(N)], axis=1).astype(ml_dtypes.bfloat16 if x.dtype != np.float64 else np.float64)
    return {"y": np.broadcast_to(o, (N,) + o.shape)}

@@ -1,0 +1,185 @@
+from concourse.bass import DstId, RemoteDMATransfer
+
+SCRATCH = {
+    "xs": ("sbuf", [128, 1280], "bfloat16"),
+    "wb": ("sbuf", [128, 640], "bfloat16"),
+    "h1a": ("sbuf", [128, 768], "bfloat16"),
+    "h1b": ("sbuf", [128, 512], "bfloat16"),
+    "h2": ("sbuf", [128, 768], "bfloat16"),
+    "ys": ("sbuf", [128, 1280], "bfloat16"),
+    "ps0": ("psum", [128, 512], "float32"),
+    "ps1": ("psum", [128, 512], "float32"),
+    "ps2": ("psum", [128, 512], "float32"),
+    "ps3": ("psum", [128, 512], "float32"),
+}
+SEMAPHORES = ["ld1", "ld2", "ldw", "a1", "aw", "a2", "a3a", "a3b", "snt", "mm0", "mm1", "mm2", "mm3", "cp", "st"]
+
+
+def _bits(m):
+    return [i for i in range(m.bit_length()) if (m >> i) & 1]
+
+
+def _mask(bs):
+    m = 0
+    for b in bs:
+        m |= 1 << b
+    return m
+
+
+def _plan(T, topo):
+    cs = list(T.cores)
+    n = len(cs)
+    F = T.x.shape[1] // n
+    K = T.w.shape[1]
+
+    def chipmates(a, b):
+        return topo.host(a) == topo.host(b) and topo.chip(a) == topo.chip(b)
+
+    C, E = [(a, b) for i, a in enumerate(cs) for b in cs[i + 1:] if chipmates(a, b)][0]
+    rest = [c for c in cs if c not in (C, E)]
+    Z = [c for c in rest if not topo.may_write(C, c)][0]
+    V = [c for c in rest if topo.same_plane(C, c)][0]
+    U = [c for c in rest if c not in (Z, V)][0]
+    order = [Z, U, C, V, E]
+    L, R = (0, 2 * F), (2 * F, 5 * F)
+    R1, R2 = (2 * F, 3 * F + F // 2), (3 * F + F // 2, 5 * F)
+    mine = {Z: L, U: L, V: R, C: R1, E: R2}
+    calls = {c: [] for c in cs}
+    expect = {}
+    sent = {c: 0 for c in cs}
+
+    def add(src, waits, items, fold=False):
+        off = [d for d, _, _, _ in items if not chipmates(src, d)]
+        on = [d for d, _, _, _ in items if chipmates(src, d)]
+        away = [p for p in cs if not chipmates(src, p) and topo.may_write(src, p)]
+        offbits = _bits(topo.mask(src, away[0]))
+        trs = []
+        for d, sem, srcs, dst in items:
+            if d in off:
+                k, m = off.index(d), len(offbits) // len(off)
+                bs = offbits[k * m:(k + 1) * m]
+            else:
+                onbits = [b for b in _bits(topo.mask(src, d)) if b not in offbits]
+                k, m = on.index(d), len(onbits) // len(on)
+                bs = onbits[k * m:(k + 1) * m]
+            trs.append((d, _mask(bs), sem, srcs, dst))
+            expect[(d, sem)] = expect.get((d, sem), 0) + len(bs)
+            sent[src] += len(bs)
+        calls[src].append((waits, trs, fold))
+
+    def rel(d, rg):
+        return rg[0] - mine[d][0], rg[1] - mine[d][0]
+
+    def x1(src, ld, pairs):
+        add(src, [ld], [(d, "a1", [("xs",) + rg], (buf,) + rel(d, rg)) for d, rg, buf in pairs])
+
+    x1(Z, "ld1", [(V, R, "h1a")])
+    x1(V, "ld1", [(Z, L, "h1a")])
+    x1(U, "ld1", [(C, R1, "h1a"), (E, R2, "h1a")])
+    x1(C, "ld1", [(U, L, "h1a")])
+    x1(E, "ld1", [(U, L, "h1b")])
+    x1(C, "ld2", [(E, R2, "h1b")])
+    x1(E, "ld2", [(C, R1, "h1b")])
+    for src, dsts in ((Z, [U]), (U, [Z]), (C, [V]), (E, [V]), (V, [C, E])):
+        s = order.index(src)
+        wr = ("wb", s * K, (s + 1) * K)
+        add(src, ["ldw"], [(d, "aw", [wr], wr) for d in dsts])
+    two = {Z: ["h1a"], V: ["h1a"], U: ["h1a", "h1b"], C: ["h1a", "h1b"], E: ["h1a", "h1b"]}
+    for src, pairs in ((Z, [(U, L)]), (U, [(Z, L)]), (V, [(C, R1), (E, R2)]), (C, [(V, R1)]), (E, [(V, R2)])):
+        add(src, ["ld2", "a1"],
+            [(d, "a2", [("xs",) + rg] + [(b,) + rel(src, rg) for b in two[src]], ("h2",) + rel(d, rg)) for d, rg in pairs],
+            fold=True)
+    got = {c: [] for c in cs}
+    for src, pairs in ((Z, [(V, "a3a")]), (V, [(Z, "a3a")]), (U, [(C, "a3a"), (E, "a3a")]),
+                       (C, [(U, "a3a"), (E, "a3b")]), (E, [(U, "a3b"), (C, "a3b")])):
+        rg = ("ys",) + mine[src]
+        add(src, ["cp"], [(d, sem, [rg], rg) for d, sem in pairs])
+        for d, sem in pairs:
+            got[d].append((sem, mine[src]))
+    return dict(F=F, K=K, order=order, mine=mine, calls=calls, expect=expect, sent=sent, got=got, two=two, L=L, R=R)
+
+
+def rank_program(g, core, T, topo):
+    if T.rank_of(core) is None:
+        return
+    p = _plan(T, topo)
+    F, K, order, sem = p["F"], p["K"], p["order"], T.sem
+    lo, hi = p["mine"][core]
+    blocks = [T.rank_of(c) for c in order]
+
+    def segs(a, b):
+        out = []
+        while a < b:
+            s = a // F
+            e = min(b, (s + 1) * F)
+            xc = blocks[s] * F + a - s * F
+            if out and out[-1][1] + out[-1][2] == xc:
+                out[-1][2] += e - a
+            else:
+                out.append([a, xc, e - a])
+            a = e
+        return out
+
+    tot = {k[1]: v for k, v in p["expect"].items() if k[0] == core}
+
+    half = p["L"] if lo < p["L"][1] else p["R"]
+    other = p["R"] if half == p["L"] else p["L"]
+    for q, name, rg in ((g.sync, "ld1", other), (g.scalar, "ld2", half)):
+        ss = segs(*rg)
+        for a, xc, m in ss:
+            q.dma_start(T.xs[:, a:a + m], T.x[:, xc:xc + m]).then_inc(sem[name], 16)
+        tot[name] = 16 * len(ss)
+    me = order.index(core)
+    g.sync.dma_start(T.wb[:, me * K:(me + 1) * K], T.w[:, :]).then_inc(sem.ldw, 16)
+    tot["ldw"] = 16
+
+    pieces = []
+    a = lo
+    while a < hi:
+        e = min(hi, (a // F + 1) * F)
+        pieces.append((a // F, a, e))
+        a = e
+    tot["cp"] = len(pieces)
+
+    te = g.tensor
+    terms = [("xs", 0, ["ld2", "ldw", "aw"])] + [(b, lo, ["a1"]) for b in p["two"][core]] + [("h2", lo, ["a2"])]
+    for t, (buf, base, waits) in enumerate(terms):
+        for s in waits:
+            te.wait_ge(sem[s], tot[s])
+        last = t == len(terms) - 1
+        for k, (s, a, e) in enumerate(pieces):
+            ins = te.matmul(T["ps%d" % k][:, 0:e - a], T.wb[:, s * K:(s + 1) * K], T[buf][:, a - base:e - base], t == 0, last)
+            if last:
+                ins.then_inc(sem["mm%d" % k], 1)
+
+    for k, (s, a, e) in enumerate(pieces):
+        g.vector.wait_ge(sem["mm%d" % k], 1)
+        g.vector.tensor_copy(T.ys[:, a:e], T["ps%d" % k][:, 0:e - a]).then_inc(sem.cp, 1)
+
+    for waits, trs, fold in p["calls"][core]:
+        for s in waits:
+            g.wait_ge(sem[s], tot[s])
+        lst = []
+        for d, m, rs, srcs, dst in trs:
+            rid, pid = topo.addr(d, core)
+            sa = [T[b][:, x0:x1] for b, x0, x1 in srcs]
+            da = T[dst[0]][:, dst[1]:dst[2]]
+            if fold:
+                lst.append(RemoteDMATransfer(dst_ids=[DstId(rid=rid, pnc=pid)], dma_engine_mask=m, remote_sem=sem[rs],
+                                             srcs=sa, dsts=[da], alu_op=1))
+            else:
+                lst.append(RemoteDMATransfer(dst_ids=[DstId(rid=rid, pnc=pid)], dma_engine_mask=m, remote_sem=sem[rs],
+                                             src=sa[0], dst=da, alu_op=0))
+        g.remote_dma_fused(lst, local_sem=sem.snt)
+
+    nst = 0
+    jobs = [(g.scalar, "cp", (lo, hi))]
+    for s, rg in p["got"][core]:
+        jobs.append((g.sync if s == "a3a" else g.scalar, s, rg))
+    for q, s, rg in jobs:
+        q.wait_ge(sem[s], tot[s])
+        for a, yc, m in segs(*rg):
+            q.dma_start(T.y[:, yc:yc + m], T.ys[:, a:a + m]).then_inc(sem.st, 16)
+            nst += 1
+    g.wait_ge(sem.snt, p["sent"][core])
+    g.wait_ge(sem.st, 16 * nst)

@@ -38,9 +38,9 @@ def _plan(T, topo):
     C, E = [(a, b) for i, a in enumerate(cs) for b in cs[i + 1:] if chipmates(a, b)][0]
     rest = [c for c in cs if c not in (C, E)]
     Z = [c for c in rest if not topo.may_write(C, c)][0]
-    V = [c for c in rest if topo.same_plane(C, c)][0]
-    U = [c for c in rest if c not in (Z, V)][0]
-    order = [Z, U, C, V, E]
+    U = [c for c in rest if topo.same_plane(C, c)][0]
+    V = [c for c in rest if c not in (Z, U)][0]
+    order = [Z, U, V, C, E]
     L, R = (0, 2 * F), (2 * F, 5 * F)
     R1, R2 = (2 * F, 3 * F + F // 2), (3 * F + F // 2, 5 * F)
     mine = {Z: L, U: L, V: R, C: R1, E: R2}
@@ -80,7 +80,7 @@ def _plan(T, topo):
     x1(E, "ld1", [(U, L, "h1b")])
     x1(C, "ld2", [(E, R2, "h1b")])
     x1(E, "ld2", [(C, R1, "h1b")])
-    for src, dsts in ((Z, [U]), (U, [Z]), (C, [V]), (E, [V]), (V, [C, E])):
+    for src, dsts in ((Z, [U]), (U, [Z]), (V, [C]), (C, [V, E]), (E, [V])):
         s = order.index(src)
         wr = ("wb", s * K, (s + 1) * K)
         add(src, ["ldw"], [(d, "aw", [wr], wr) for d in dsts])
@@ -124,13 +124,19 @@ def rank_program(g, core, T, topo):
 
     half = p["L"] if lo < p["L"][1] else p["R"]
     other = p["R"] if half == p["L"] else p["L"]
-    for q, name, rg in ((g.sync, "ld1", other), (g.scalar, "ld2", half)):
+    qs, nq = (g.sync, g.scalar), [0]
+
+    def nextq():
+        nq[0] += 1
+        return qs[(nq[0] - 1) % len(qs)]
+
+    for name, rg in (("ld1", other), ("ld2", half)):
         ss = segs(*rg)
         for a, xc, m in ss:
-            q.dma_start(T.xs[:, a:a + m], T.x[:, xc:xc + m]).then_inc(sem[name], 16)
+            nextq().dma_start(T.xs[:, a:a + m], T.x[:, xc:xc + m]).then_inc(sem[name], 16)
         tot[name] = 16 * len(ss)
     me = order.index(core)
-    g.sync.dma_start(T.wb[:, me * K:(me + 1) * K], T.w[:, :]).then_inc(sem.ldw, 16)
+    nextq().dma_start(T.wb[:, me * K:(me + 1) * K], T.w[:, :]).then_inc(sem.ldw, 16)
     tot["ldw"] = 16
 
     pieces = []
@@ -173,12 +179,11 @@ def rank_program(g, core, T, topo):
         g.remote_dma_fused(lst, local_sem=sem.snt)
 
     nst = 0
-    jobs = [(g.scalar, "cp", (lo, hi))]
-    for s, rg in p["got"][core]:
-        jobs.append((g.sync if s == "a3a" else g.scalar, s, rg))
-    for q, s, rg in jobs:
-        q.wait_ge(sem[s], tot[s])
+    jobs = [("cp", (lo, hi))] + sorted(p["got"][core], reverse=True)
+    for s, rg in jobs:
         for a, yc, m in segs(*rg):
+            q = nextq()
+            q.wait_ge(sem[s], tot[s])
             q.dma_start(T.y[:, yc:yc + m], T.ys[:, a:a + m]).then_inc(sem.st, 16)
             nst += 1
     g.wait_ge(sem.snt, p["sent"][core])

@@ -3,16 +3,15 @@ from concourse.bass import DstId, RemoteDMATransfer
 SCRATCH = {
     "xs": ("sbuf", [128, 1280], "bfloat16"),
     "wb": ("sbuf", [128, 640], "bfloat16"),
-    "h1a": ("sbuf", [128, 768], "bfloat16"),
-    "h1b": ("sbuf", [128, 512], "bfloat16"),
-    "h2": ("sbuf", [128, 768], "bfloat16"),
+    "h1a": ("sbuf", [128, 384], "bfloat16"),
+    "h1b": ("sbuf", [128, 384], "bfloat16"),
+    "h1c": ("sbuf", [128, 256], "bfloat16"),
+    "h2": ("sbuf", [128, 384], "bfloat16"),
     "ys": ("sbuf", [128, 1280], "bfloat16"),
     "ps0": ("psum", [128, 512], "float32"),
     "ps1": ("psum", [128, 512], "float32"),
-    "ps2": ("psum", [128, 512], "float32"),
-    "ps3": ("psum", [128, 512], "float32"),
 }
-SEMAPHORES = ["ld1", "ld2", "ldw", "a1", "aw", "a2", "a3a", "a3b", "snt", "mm0", "mm1", "mm2", "mm3", "cp", "st"]
+SEMAPHORES = ["ld1", "ld2", "ldw", "a1", "aw", "a2", "a3a", "a3b", "a3c", "snt", "mm0", "mm1", "cp", "st"]
 
 
 def _bits(m):
@@ -29,8 +28,8 @@ def _mask(bs):
 def _plan(T, topo):
     cs = list(T.cores)
     n = len(cs)
-    F = T.x.shape[1] // n
-    K = T.w.shape[1]
+    F = T.xs.shape[1] // n
+    K = T.wb.shape[1] // n
 
     def chipmates(a, b):
         return topo.host(a) == topo.host(b) and topo.chip(a) == topo.chip(b)
@@ -40,13 +39,17 @@ def _plan(T, topo):
     Z = [c for c in rest if not topo.may_write(C, c)][0]
     U = [c for c in rest if topo.same_plane(C, c)][0]
     V = [c for c in rest if c not in (Z, U)][0]
+    Zh, Uh, Vh = Z + E - C, U + E - C, V + E - C
     order = [Z, U, V, C, E]
     L, R = (0, 2 * F), (2 * F, 5 * F)
+    L1, L2 = (0, F), (F, 2 * F)
     R1, R2 = (2 * F, 3 * F + F // 2), (3 * F + F // 2, 5 * F)
-    mine = {Z: L, U: L, V: R, C: R1, E: R2}
-    calls = {c: [] for c in cs}
+    mine = {Z: L1, U: L1, Zh: L2, Uh: L2, V: R1, C: R1, Vh: R2, E: R2}
+    partner = {Z: U, U: Z, Zh: Uh, Uh: Zh, V: C, C: V, Vh: E, E: Vh}
+    racks = (([Z, V], [Z, Zh, V, Vh]), ([U, C, E], [U, Uh, C, E]))
+    calls = {c: [] for c in mine}
     expect = {}
-    sent = {c: 0 for c in cs}
+    sent = {c: 0 for c in mine}
 
     def add(src, waits, items, fold=False):
         off = [d for d, _, _, _ in items if not chipmates(src, d)]
@@ -67,42 +70,54 @@ def _plan(T, topo):
             sent[src] += len(bs)
         calls[src].append((waits, trs, fold))
 
-    def rel(d, rg):
-        return rg[0] - mine[d][0], rg[1] - mine[d][0]
+    land = {c: [] for c in mine}
 
-    def x1(src, ld, pairs):
-        add(src, [ld], [(d, "a1", [("xs",) + rg], (buf,) + rel(d, rg)) for d, rg, buf in pairs])
+    def x1(src, ld, dsts):
+        items = []
+        for d in dsts:
+            buf = "h1" + "abc"[len(land[d])]
+            land[d].append(buf)
+            items.append((d, "a1", [("xs",) + mine[d]], (buf, 0, mine[d][1] - mine[d][0])))
+        add(src, [ld], items)
 
-    x1(Z, "ld1", [(V, R, "h1a")])
-    x1(V, "ld1", [(Z, L, "h1a")])
-    x1(U, "ld1", [(C, R1, "h1a"), (E, R2, "h1a")])
-    x1(C, "ld1", [(U, L, "h1a")])
-    x1(E, "ld1", [(U, L, "h1b")])
-    x1(C, "ld2", [(E, R2, "h1b")])
-    x1(E, "ld2", [(C, R1, "h1b")])
-    for src, dsts in ((Z, [U]), (U, [Z]), (V, [C]), (C, [V, E]), (E, [V])):
-        s = order.index(src)
+    for ranks, fins in racks:
+        for r in ranks:
+            x1(r, "ld1", [f for f in fins if not chipmates(r, f)])
+    for ranks, fins in racks:
+        for r in ranks:
+            x1(r, "ld2", [f for f in fins if chipmates(r, f) and f != r])
+
+    def wsend(src, owner, dsts, waits):
+        s = order.index(owner)
         wr = ("wb", s * K, (s + 1) * K)
-        add(src, ["ldw"], [(d, "aw", [wr], wr) for d in dsts])
-    two = {Z: ["h1a"], V: ["h1a"], U: ["h1a", "h1b"], C: ["h1a", "h1b"], E: ["h1a", "h1b"]}
-    for src, pairs in ((Z, [(U, L)]), (U, [(Z, L)]), (V, [(C, R1), (E, R2)]), (C, [(V, R1)]), (E, [(V, R2)])):
-        add(src, ["ld2", "a1"],
-            [(d, "a2", [("xs",) + rg] + [(b,) + rel(src, rg) for b in two[src]], ("h2",) + rel(d, rg)) for d, rg in pairs],
-            fold=True)
+        add(src, waits, [(d, "aw", [wr], wr) for d in dsts])
+
+    for src, dsts in ((Z, [U]), (U, [Zh, Uh]), (V, [C]), (C, [V, E]), (E, [Vh])):
+        wsend(src, src, dsts, ["ldw"])
+    for f in mine:
+        wd = mine[f][1] - mine[f][0]
+        srcs = ([("xs",) + mine[f]] if f in cs else []) + [(b, 0, wd) for b in land[f]]
+        add(f, ["ld2", "a1"], [(partner[f], "a2", srcs, ("h2", 0, wd))], fold=True)
+    wsend(V, C, [Vh], ["aw"])
     got = {c: [] for c in cs}
-    for src, pairs in ((Z, [(V, "a3a")]), (V, [(Z, "a3a")]), (U, [(C, "a3a"), (E, "a3a")]),
-                       (C, [(U, "a3a"), (E, "a3b")]), (E, [(U, "a3b"), (C, "a3b")])):
-        rg = ("ys",) + mine[src]
-        add(src, ["cp"], [(d, sem, [rg], rg) for d, sem in pairs])
-        for d, sem in pairs:
-            got[d].append((sem, mine[src]))
-    return dict(F=F, K=K, order=order, mine=mine, calls=calls, expect=expect, sent=sent, got=got, two=two, L=L, R=R)
+    for ranks, fins in racks:
+        for f in fins:
+            rg = ("ys",) + mine[f]
+            items = []
+            for d in ranks:
+                if d != f:
+                    sem = "a3" + "abc"[len(got[d])]
+                    got[d].append((0 if chipmates(f, d) else 1, sem, mine[f]))
+                    items.append((d, sem, [rg], rg))
+            add(f, ["cp"], items)
+    return dict(F=F, K=K, order=order, mine=mine, calls=calls, expect=expect, sent=sent, got=got, land=land, L=L, R=R)
 
 
 def rank_program(g, core, T, topo):
-    if T.rank_of(core) is None:
-        return
     p = _plan(T, topo)
+    if core not in p["mine"]:
+        return
+    isrank = T.rank_of(core) is not None
     F, K, order, sem = p["F"], p["K"], p["order"], T.sem
     lo, hi = p["mine"][core]
     blocks = [T.rank_of(c) for c in order]
@@ -121,23 +136,23 @@ def rank_program(g, core, T, topo):
         return out
 
     tot = {k[1]: v for k, v in p["expect"].items() if k[0] == core}
-
-    half = p["L"] if lo < p["L"][1] else p["R"]
-    other = p["R"] if half == p["L"] else p["L"]
     qs, nq = (g.sync, g.scalar), [0]
 
     def nextq():
         nq[0] += 1
         return qs[(nq[0] - 1) % len(qs)]
 
-    for name, rg in (("ld1", other), ("ld2", half)):
-        ss = segs(*rg)
-        for a, xc, m in ss:
-            nextq().dma_start(T.xs[:, a:a + m], T.x[:, xc:xc + m]).then_inc(sem[name], 16)
-        tot[name] = 16 * len(ss)
-    me = order.index(core)
-    nextq().dma_start(T.wb[:, me * K:(me + 1) * K], T.w[:, :]).then_inc(sem.ldw, 16)
-    tot["ldw"] = 16
+    if isrank:
+        half = p["L"] if lo < p["L"][1] else p["R"]
+        other = p["R"] if half == p["L"] else p["L"]
+        for name, rg in (("ld1", other), ("ld2", half)):
+            ss = segs(*rg)
+            for a, xc, m in ss:
+                nextq().dma_start(T.xs[:, a:a + m], T.x[:, xc:xc + m]).then_inc(sem[name], 16)
+            tot[name] = 16 * len(ss)
+        me = order.index(core)
+        nextq().dma_start(T.wb[:, me * K:(me + 1) * K], T.w[:, :]).then_inc(sem.ldw, 16)
+        tot["ldw"] = 16
 
     pieces = []
     a = lo
@@ -148,10 +163,11 @@ def rank_program(g, core, T, topo):
     tot["cp"] = len(pieces)
 
     te = g.tensor
-    terms = [("xs", 0, ["ld2", "ldw", "aw"])] + [(b, lo, ["a1"]) for b in p["two"][core]] + [("h2", lo, ["a2"])]
+    terms = ([("xs", 0, ["ld2", "ldw"])] if isrank else []) + [(b, lo, ["a1"]) for b in p["land"][core]] + [("h2", lo, ["a2"])]
     for t, (buf, base, waits) in enumerate(terms):
-        for s in waits:
-            te.wait_ge(sem[s], tot[s])
+        for s in waits + (["aw"] if t == 0 else []):
+            if s in tot:
+                te.wait_ge(sem[s], tot[s])
         last = t == len(terms) - 1
         for k, (s, a, e) in enumerate(pieces):
             ins = te.matmul(T["ps%d" % k][:, 0:e - a], T.wb[:, s * K:(s + 1) * K], T[buf][:, a - base:e - base], t == 0, last)
@@ -164,7 +180,8 @@ def rank_program(g, core, T, topo):
 
     for waits, trs, fold in p["calls"][core]:
         for s in waits:
-            g.wait_ge(sem[s], tot[s])
+            if s in tot:
+                g.wait_ge(sem[s], tot[s])
         lst = []
         for d, m, rs, srcs, dst in trs:
             rid, pid = topo.addr(d, core)
@@ -179,12 +196,14 @@ def rank_program(g, core, T, topo):
         g.remote_dma_fused(lst, local_sem=sem.snt)
 
     nst = 0
-    jobs = [("cp", (lo, hi))] + sorted(p["got"][core], reverse=True)
-    for s, rg in jobs:
-        for a, yc, m in segs(*rg):
-            q = nextq()
-            q.wait_ge(sem[s], tot[s])
-            q.dma_start(T.y[:, yc:yc + m], T.ys[:, a:a + m]).then_inc(sem.st, 16)
-            nst += 1
+    if isrank:
+        jobs = [("cp", (lo, hi))] + [(s, rg) for _, s, rg in sorted(p["got"][core])]
+        for s, rg in jobs:
+            for a, yc, m in segs(*rg):
+                q = nextq()
+                q.wait_ge(sem[s], tot[s])
+                q.dma_start(T.y[:, yc:yc + m], T.ys[:, a:a + m]).then_inc(sem.st, 16)
+                nst += 1
     g.wait_ge(sem.snt, p["sent"][core])
-    g.wait_ge(sem.st, 16 * nst)
+    if nst:
+        g.wait_ge(sem.st, 16 * nst)

@@ -3,15 +3,14 @@ from concourse.bass import DstId, RemoteDMATransfer
 SCRATCH = {
     "xs": ("sbuf", [128, 1280], "bfloat16"),
     "wb": ("sbuf", [128, 640], "bfloat16"),
-    "h1a": ("sbuf", [128, 384], "bfloat16"),
-    "h1b": ("sbuf", [128, 384], "bfloat16"),
+    "h1a": ("sbuf", [128, 256], "bfloat16"),
+    "h1b": ("sbuf", [128, 256], "bfloat16"),
     "h1c": ("sbuf", [128, 256], "bfloat16"),
-    "h2": ("sbuf", [128, 384], "bfloat16"),
+    "h2": ("sbuf", [128, 256], "bfloat16"),
     "ys": ("sbuf", [128, 1280], "bfloat16"),
     "ps0": ("psum", [128, 512], "float32"),
-    "ps1": ("psum", [128, 512], "float32"),
 }
-SEMAPHORES = ["ld1", "ld2", "ldw", "a1", "aw", "a2", "a3a", "a3b", "a3c", "snt", "mm0", "mm1", "cp", "st"]
+SEMAPHORES = ["ld1", "ld2", "ldw", "a1", "aw", "a2", "a3a", "a3b", "a3c", "a3d", "snt", "mm0", "cp", "st"]
 
 
 def _bits(m):
@@ -34,19 +33,25 @@ def _plan(T, topo):
     def chipmates(a, b):
         return topo.host(a) == topo.host(b) and topo.chip(a) == topo.chip(b)
 
+    def otherdie(c):
+        w = topo.CORES_PER_CHIP
+        return [d for d in range(max(0, c - w), c + w) if chipmates(c, d) and topo.die(d) != topo.die(c)][0]
+
     C, E = [(a, b) for i, a in enumerate(cs) for b in cs[i + 1:] if chipmates(a, b)][0]
     rest = [c for c in cs if c not in (C, E)]
     Z = [c for c in rest if not topo.may_write(C, c)][0]
     U = [c for c in rest if topo.same_plane(C, c)][0]
     V = [c for c in rest if c not in (Z, U)][0]
     Zh, Uh, Vh = Z + E - C, U + E - C, V + E - C
+    Vg, H = otherdie(V), otherdie(C)
     order = [Z, U, V, C, E]
     L, R = (0, 2 * F), (2 * F, 5 * F)
-    L1, L2 = (0, F), (F, 2 * F)
-    R1, R2 = (2 * F, 3 * F + F // 2), (3 * F + F // 2, 5 * F)
-    mine = {Z: L1, U: L1, Zh: L2, Uh: L2, V: R1, C: R1, Vh: R2, E: R2}
-    partner = {Z: U, U: Z, Zh: Uh, Uh: Zh, V: C, C: V, Vh: E, E: Vh}
-    racks = (([Z, V], [Z, Zh, V, Vh]), ([U, C, E], [U, Uh, C, E]))
+    lanes = ((Z, U), (Zh, Uh), (V, H), (Vh, C), (Vg, E))
+    mine, partner = {}, {}
+    for s, (a, b) in enumerate(lanes):
+        mine[a] = mine[b] = (s * F, (s + 1) * F)
+        partner[a], partner[b] = b, a
+    racks = (([Z, V], [a for a, _ in lanes]), ([U, C, E], [b for _, b in lanes]))
     calls = {c: [] for c in mine}
     expect = {}
     sent = {c: 0 for c in mine}
@@ -77,28 +82,26 @@ def _plan(T, topo):
         for d in dsts:
             buf = "h1" + "abc"[len(land[d])]
             land[d].append(buf)
-            items.append((d, "a1", [("xs",) + mine[d]], (buf, 0, mine[d][1] - mine[d][0])))
+            items.append((d, "a1", [("xs",) + mine[d]], (buf, 0, F)))
         add(src, [ld], items)
 
     for ranks, fins in racks:
         for r in ranks:
-            x1(r, "ld1", [f for f in fins if not chipmates(r, f)])
-    for ranks, fins in racks:
-        for r in ranks:
-            x1(r, "ld2", [f for f in fins if chipmates(r, f) and f != r])
-
-    def wsend(src, owner, dsts, waits):
-        s = order.index(owner)
+            off = [f for f in fins if not chipmates(r, f)]
+            on = [f for f in fins if chipmates(r, f) and f != r]
+            if len(_bits(len(off))) == 1:
+                x1(r, "ld1", off)
+                x1(r, "ld2", on)
+            else:
+                x1(r, "ld1", [f for f in off if f not in cs])
+                x1(r, "ld2", on)
+                x1(r, "ld1", [f for f in off if f in cs])
+    for s, src in enumerate(order):
         wr = ("wb", s * K, (s + 1) * K)
-        add(src, waits, [(d, "aw", [wr], wr) for d in dsts])
-
-    for src, dsts in ((Z, [U]), (U, [Zh, Uh]), (V, [C]), (C, [V, E]), (E, [Vh])):
-        wsend(src, src, dsts, ["ldw"])
+        add(src, ["ldw"], [(d, "aw", [wr], wr) for d in lanes[s] if d != src])
     for f in mine:
-        wd = mine[f][1] - mine[f][0]
-        srcs = ([("xs",) + mine[f]] if f in cs else []) + [(b, 0, wd) for b in land[f]]
-        add(f, ["ld2", "a1"], [(partner[f], "a2", srcs, ("h2", 0, wd))], fold=True)
-    wsend(V, C, [Vh], ["aw"])
+        srcs = ([("xs",) + mine[f]] if f in cs else []) + [(b, 0, F) for b in land[f]]
+        add(f, ["ld2", "a1"], [(partner[f], "a2", srcs, ("h2", 0, F))], fold=True)
     got = {c: [] for c in cs}
     for ranks, fins in racks:
         for f in fins:
@@ -106,7 +109,7 @@ def _plan(T, topo):
             items = []
             for d in ranks:
                 if d != f:
-                    sem = "a3" + "abc"[len(got[d])]
+                    sem = "a3" + "abcd"[len(got[d])]
                     got[d].append((0 if chipmates(f, d) else 1, sem, mine[f]))
                     items.append((d, sem, [rg], rg))
             add(f, ["cp"], items)
@@ -153,35 +156,27 @@ def rank_program(g, core, T, topo):
         me = order.index(core)
         nextq().dma_start(T.wb[:, me * K:(me + 1) * K], T.w[:, :]).then_inc(sem.ldw, 16)
         tot["ldw"] = 16
-
-    pieces = []
-    a = lo
-    while a < hi:
-        e = min(hi, (a // F + 1) * F)
-        pieces.append((a // F, a, e))
-        a = e
-    tot["cp"] = len(pieces)
+    tot["cp"] = 1
 
     te = g.tensor
+    s = lo // F
     terms = ([("xs", 0, ["ld2", "ldw"])] if isrank else []) + [(b, lo, ["a1"]) for b in p["land"][core]] + [("h2", lo, ["a2"])]
     for t, (buf, base, waits) in enumerate(terms):
-        for s in waits + (["aw"] if t == 0 else []):
-            if s in tot:
-                te.wait_ge(sem[s], tot[s])
+        for q in waits + (["aw"] if t == 0 else []):
+            if q in tot:
+                te.wait_ge(sem[q], tot[q])
         last = t == len(terms) - 1
-        for k, (s, a, e) in enumerate(pieces):
-            ins = te.matmul(T["ps%d" % k][:, 0:e - a], T.wb[:, s * K:(s + 1) * K], T[buf][:, a - base:e - base], t == 0, last)
-            if last:
-                ins.then_inc(sem["mm%d" % k], 1)
+        ins = te.matmul(T.ps0[:, 0:F], T.wb[:, s * K:(s + 1) * K], T[buf][:, lo - base:hi - base], t == 0, last)
+        if last:
+            ins.then_inc(sem.mm0, 1)
 
-    for k, (s, a, e) in enumerate(pieces):
-        g.vector.wait_ge(sem["mm%d" % k], 1)
-        g.vector.tensor_copy(T.ys[:, a:e], T["ps%d" % k][:, 0:e - a]).then_inc(sem.cp, 1)
+    g.vector.wait_ge(sem.mm0, 1)
+    g.vector.tensor_copy(T.ys[:, lo:hi], T.ps0[:, 0:F]).then_inc(sem.cp, 1)
 
     for waits, trs, fold in p["calls"][core]:
-        for s in waits:
-            if s in tot:
-                g.wait_ge(sem[s], tot[s])
+        for q in waits:
+            if q in tot:
+                g.wait_ge(sem[q], tot[q])
         lst = []
         for d, m, rs, srcs, dst in trs:
             rid, pid = topo.addr(d, core)
@@ -197,12 +192,12 @@ def rank_program(g, core, T, topo):
 
     nst = 0
     if isrank:
-        jobs = [("cp", (lo, hi))] + [(s, rg) for _, s, rg in sorted(p["got"][core])]
-        for s, rg in jobs:
+        jobs = [("cp", (lo, hi))] + [(q, rg) for _, q, rg in sorted(p["got"][core])]
+        for q, rg in jobs:
             for a, yc, m in segs(*rg):
-                q = nextq()
-                q.wait_ge(sem[s], tot[s])
-                q.dma_start(T.y[:, yc:yc + m], T.ys[:, a:a + m]).then_inc(sem.st, 16)
+                dq = nextq()
+                dq.wait_ge(sem[q], tot[q])
+                dq.dma_start(T.y[:, yc:yc + m], T.ys[:, a:a + m]).then_inc(sem.st, 16)
                 nst += 1
     g.wait_ge(sem.snt, p["sent"][core])
     if nst:

@@ -9,8 +9,11 @@ SCRATCH = {
     "h2": ("sbuf", [128, 256], "bfloat16"),
     "ys": ("sbuf", [128, 1280], "bfloat16"),
     "ps0": ("psum", [128, 512], "float32"),
+    "ps1": ("psum", [128, 512], "float32"),
 }
-SEMAPHORES = ["ld1", "ld2", "ldw", "a1", "aw", "a2", "a3a", "a3b", "a3c", "a3d", "snt", "mm0", "cp", "st"]
+SEMAPHORES = (["ld1", "ld2", "ldw", "a1", "aw", "a20", "a21", "snt", "mm0", "mm1", "cp0", "cp1", "st"]
+              + ["a3%s%d" % (k, h) for k in "abcde" for h in range(2)])
+PARTS = 2
 
 
 def _bits(m):
@@ -46,7 +49,7 @@ def _plan(T, topo):
     Vg, H = otherdie(V), otherdie(C)
     order = [Z, U, V, C, E]
     L, R = (0, 2 * F), (2 * F, 5 * F)
-    lanes = ((Z, U), (Zh, Uh), (V, H), (Vh, C), (Vg, E))
+    lanes = ((Z, Uh), (Zh, U), (V, H), (Vh, C), (Vg, E))
     mine, partner = {}, {}
     for s, (a, b) in enumerate(lanes):
         mine[a] = mine[b] = (s * F, (s + 1) * F)
@@ -99,20 +102,25 @@ def _plan(T, topo):
     for s, src in enumerate(order):
         wr = ("wb", s * K, (s + 1) * K)
         add(src, ["ldw"], [(d, "aw", [wr], wr) for d in lanes[s] if d != src])
-    for f in mine:
-        srcs = ([("xs",) + mine[f]] if f in cs else []) + [(b, 0, F) for b in land[f]]
-        add(f, ["ld2", "a1"], [(partner[f], "a2", srcs, ("h2", 0, F))], fold=True)
+    Hf = F // PARTS
+    for h in range(PARTS):
+        for f in mine:
+            lo = mine[f][0]
+            srcs = ([("xs", lo + h * Hf, lo + (h + 1) * Hf)] if f in cs else []) + [(b, h * Hf, (h + 1) * Hf) for b in land[f]]
+            add(f, ["ld2", "a1"], [(partner[f], "a2%d" % h, srcs, ("h2", h * Hf, (h + 1) * Hf))], fold=True)
     got = {c: [] for c in cs}
-    for ranks, fins in racks:
-        for f in fins:
-            rg = ("ys",) + mine[f]
-            items = []
-            for d in ranks:
-                if d != f:
-                    sem = "a3" + "abcd"[len(got[d])]
-                    got[d].append((0 if chipmates(f, d) else 1, sem, mine[f]))
-                    items.append((d, sem, [rg], rg))
-            add(f, ["cp"], items)
+    for h in range(PARTS):
+        for ranks, fins in racks:
+            for k, f in enumerate(fins):
+                lo = mine[f][0]
+                rg = ("ys", lo + h * Hf, lo + (h + 1) * Hf)
+                items = []
+                for d in ranks:
+                    if d != f:
+                        sem = "a3%s%d" % ("abcde"[k], h)
+                        got[d].append((h, 0 if chipmates(f, d) else 1, sem, rg[1:]))
+                        items.append((d, sem, [rg], rg))
+                add(f, ["cp%d" % h], items)
     return dict(F=F, K=K, order=order, mine=mine, calls=calls, expect=expect, sent=sent, got=got, land=land, L=L, R=R)
 
 
@@ -156,22 +164,28 @@ def rank_program(g, core, T, topo):
         me = order.index(core)
         nextq().dma_start(T.wb[:, me * K:(me + 1) * K], T.w[:, :]).then_inc(sem.ldw, 16)
         tot["ldw"] = 16
-    tot["cp"] = 1
+    Hf = F // PARTS
+    for h in range(PARTS):
+        tot["cp%d" % h] = 1
 
     te = g.tensor
     s = lo // F
-    terms = ([("xs", 0, ["ld2", "ldw"])] if isrank else []) + [(b, lo, ["a1"]) for b in p["land"][core]] + [("h2", lo, ["a2"])]
+    wsl = T.wb[:, s * K:(s + 1) * K]
+    terms = ([("xs", 0, ["ld2", "ldw"])] if isrank else []) + [(b, lo, ["a1"]) for b in p["land"][core]]
     for t, (buf, base, waits) in enumerate(terms):
         for q in waits + (["aw"] if t == 0 else []):
             if q in tot:
                 te.wait_ge(sem[q], tot[q])
-        last = t == len(terms) - 1
-        ins = te.matmul(T.ps0[:, 0:F], T.wb[:, s * K:(s + 1) * K], T[buf][:, lo - base:hi - base], t == 0, last)
-        if last:
-            ins.then_inc(sem.mm0, 1)
+        for h in range(PARTS):
+            a = lo - base + h * Hf
+            te.matmul(T["ps%d" % h][:, 0:Hf], wsl, T[buf][:, a:a + Hf], t == 0, False)
+    for h in range(PARTS):
+        te.wait_ge(sem["a2%d" % h], tot["a2%d" % h])
+        te.matmul(T["ps%d" % h][:, 0:Hf], wsl, T.h2[:, h * Hf:(h + 1) * Hf], False, True).then_inc(sem["mm%d" % h], 1)
 
-    g.vector.wait_ge(sem.mm0, 1)
-    g.vector.tensor_copy(T.ys[:, lo:hi], T.ps0[:, 0:F]).then_inc(sem.cp, 1)
+    for h in range(PARTS):
+        g.vector.wait_ge(sem["mm%d" % h], 1)
+        g.vector.tensor_copy(T.ys[:, lo + h * Hf:lo + (h + 1) * Hf], T["ps%d" % h][:, 0:Hf]).then_inc(sem["cp%d" % h], 1)
 
     for waits, trs, fold in p["calls"][core]:
         for q in waits:
@@ -192,7 +206,8 @@ def rank_program(g, core, T, topo):
 
     nst = 0
     if isrank:
-        jobs = [("cp", (lo, hi))] + [(q, rg) for _, q, rg in sorted(p["got"][core])]
+        own = [(h, -1, "cp%d" % h, (lo + h * Hf, lo + (h + 1) * Hf)) for h in range(PARTS)]
+        jobs = [(q, rg) for _, _, q, rg in sorted(own + p["got"][core])]
         for q, rg in jobs:
             for a, yc, m in segs(*rg):
                 dq = nextq()

from concourse.bass import DstId, RemoteDMATransfer

SCRATCH = {
    "xs": ("sbuf", [128, 1280], "bfloat16"),
    "wb": ("sbuf", [128, 640], "bfloat16"),
    "h1a": ("sbuf", [128, 256], "bfloat16"),
    "h1b": ("sbuf", [128, 256], "bfloat16"),
    "h1c": ("sbuf", [128, 256], "bfloat16"),
    "h2": ("sbuf", [128, 256], "bfloat16"),
    "ys": ("sbuf", [128, 1280], "bfloat16"),
    "ps0": ("psum", [128, 512], "float32"),
    "ps1": ("psum", [128, 512], "float32"),
}
SEMAPHORES = (["ld1", "ld2", "ldw", "a1", "aw", "a20", "a21", "snt", "mm0", "mm1", "cp0", "cp1", "st"]
              + ["a3%s%d" % (k, h) for k in "abcde" for h in range(2)])
PARTS = 2


def _bits(m):
    return [i for i in range(m.bit_length()) if (m >> i) & 1]


def _mask(bs):
    m = 0
    for b in bs:
        m |= 1 << b
    return m


def _plan(T, topo):
    cs = list(T.cores)
    n = len(cs)
    F = T.xs.shape[1] // n
    K = T.wb.shape[1] // n

    def chipmates(a, b):
        return topo.host(a) == topo.host(b) and topo.chip(a) == topo.chip(b)

    def otherdie(c):
        w = topo.CORES_PER_CHIP
        return [d for d in range(max(0, c - w), c + w) if chipmates(c, d) and topo.die(d) != topo.die(c)][0]

    C, E = [(a, b) for i, a in enumerate(cs) for b in cs[i + 1:] if chipmates(a, b)][0]
    rest = [c for c in cs if c not in (C, E)]
    Z = [c for c in rest if not topo.may_write(C, c)][0]
    U = [c for c in rest if topo.same_plane(C, c)][0]
    V = [c for c in rest if c not in (Z, U)][0]
    Zh, Uh, Vh = Z + E - C, U + E - C, V + E - C
    Vg, H = otherdie(V), otherdie(C)
    order = [Z, U, V, C, E]
    L, R = (0, 2 * F), (2 * F, 5 * F)
    lanes = ((Z, Uh), (Zh, U), (V, H), (Vh, C), (Vg, E))
    mine, partner = {}, {}
    for s, (a, b) in enumerate(lanes):
        mine[a] = mine[b] = (s * F, (s + 1) * F)
        partner[a], partner[b] = b, a
    racks = (([Z, V], [a for a, _ in lanes]), ([U, C, E], [b for _, b in lanes]))
    calls = {c: [] for c in mine}
    expect = {}
    sent = {c: 0 for c in mine}

    def add(src, waits, items, fold=False):
        off = [d for d, _, _, _ in items if not chipmates(src, d)]
        on = [d for d, _, _, _ in items if chipmates(src, d)]
        away = [p for p in cs if not chipmates(src, p) and topo.may_write(src, p)]
        offbits = _bits(topo.mask(src, away[0]))
        trs = []
        for d, sem, srcs, dst in items:
            if d in off:
                k, m = off.index(d), len(offbits) // len(off)
                bs = offbits[k * m:(k + 1) * m]
            else:
                onbits = [b for b in _bits(topo.mask(src, d)) if b not in offbits]
                k, m = on.index(d), len(onbits) // len(on)
                bs = onbits[k * m:(k + 1) * m]
            trs.append((d, _mask(bs), sem, srcs, dst))
            expect[(d, sem)] = expect.get((d, sem), 0) + len(bs)
            sent[src] += len(bs)
        calls[src].append((waits, trs, fold))

    land = {c: [] for c in mine}

    def x1(src, ld, dsts):
        items = []
        for d in dsts:
            buf = "h1" + "abc"[len(land[d])]
            land[d].append(buf)
            items.append((d, "a1", [("xs",) + mine[d]], (buf, 0, F)))
        add(src, [ld], items)

    for ranks, fins in racks:
        for r in ranks:
            off = [f for f in fins if not chipmates(r, f)]
            on = [f for f in fins if chipmates(r, f) and f != r]
            if len(_bits(len(off))) == 1:
                x1(r, "ld1", off)
                x1(r, "ld2", on)
            else:
                x1(r, "ld1", [f for f in off if f not in cs])
                x1(r, "ld2", on)
                x1(r, "ld1", [f for f in off if f in cs])
    for s, src in enumerate(order):
        wr = ("wb", s * K, (s + 1) * K)
        add(src, ["ldw"], [(d, "aw", [wr], wr) for d in lanes[s] if d != src])
    Hf = F // PARTS
    for h in range(PARTS):
        for f in mine:
            lo = mine[f][0]
            srcs = ([("xs", lo + h * Hf, lo + (h + 1) * Hf)] if f in cs else []) + [(b, h * Hf, (h + 1) * Hf) for b in land[f]]
            add(f, ["ld2", "a1"], [(partner[f], "a2%d" % h, srcs, ("h2", h * Hf, (h + 1) * Hf))], fold=True)
    got = {c: [] for c in cs}
    for h in range(PARTS):
        for ranks, fins in racks:
            for k, f in enumerate(fins):
                lo = mine[f][0]
                rg = ("ys", lo + h * Hf, lo + (h + 1) * Hf)
                items = []
                for d in ranks:
                    if d != f:
                        sem = "a3%s%d" % ("abcde"[k], h)
                        got[d].append((h, 0 if chipmates(f, d) else 1, sem, rg[1:]))
                        items.append((d, sem, [rg], rg))
                add(f, ["cp%d" % h], items)
    return dict(F=F, K=K, order=order, mine=mine, calls=calls, expect=expect, sent=sent, got=got, land=land, L=L, R=R)


def rank_program(g, core, T, topo):
    p = _plan(T, topo)
    if core not in p["mine"]:
        return
    isrank = T.rank_of(core) is not None
    F, K, order, sem = p["F"], p["K"], p["order"], T.sem
    lo, hi = p["mine"][core]
    blocks = [T.rank_of(c) for c in order]

    def segs(a, b):
        out = []
        while a < b:
            s = a // F
            e = min(b, (s + 1) * F)
            xc = blocks[s] * F + a - s * F
            if out and out[-1][1] + out[-1][2] == xc:
                out[-1][2] += e - a
            else:
                out.append([a, xc, e - a])
            a = e
        return out

    tot = {k[1]: v for k, v in p["expect"].items() if k[0] == core}
    qs, nq = (g.sync, g.scalar), [0]

    def nextq():
        nq[0] += 1
        return qs[(nq[0] - 1) % len(qs)]

    if isrank:
        half = p["L"] if lo < p["L"][1] else p["R"]
        other = p["R"] if half == p["L"] else p["L"]
        for name, rg in (("ld1", other), ("ld2", half)):
            ss = segs(*rg)
            for a, xc, m in ss:
                nextq().dma_start(T.xs[:, a:a + m], T.x[:, xc:xc + m]).then_inc(sem[name], 16)
            tot[name] = 16 * len(ss)
        me = order.index(core)
        nextq().dma_start(T.wb[:, me * K:(me + 1) * K], T.w[:, :]).then_inc(sem.ldw, 16)
        tot["ldw"] = 16
    Hf = F // PARTS
    for h in range(PARTS):
        tot["cp%d" % h] = 1

    te = g.tensor
    s = lo // F
    wsl = T.wb[:, s * K:(s + 1) * K]
    terms = ([("xs", 0, ["ld2", "ldw"])] if isrank else []) + [(b, lo, ["a1"]) for b in p["land"][core]]
    for t, (buf, base, waits) in enumerate(terms):
        for q in waits + (["aw"] if t == 0 else []):
            if q in tot:
                te.wait_ge(sem[q], tot[q])
        for h in range(PARTS):
            a = lo - base + h * Hf
            te.matmul(T["ps%d" % h][:, 0:Hf], wsl, T[buf][:, a:a + Hf], t == 0, False)
    for h in range(PARTS):
        te.wait_ge(sem["a2%d" % h], tot["a2%d" % h])
        te.matmul(T["ps%d" % h][:, 0:Hf], wsl, T.h2[:, h * Hf:(h + 1) * Hf], False, True).then_inc(sem["mm%d" % h], 1)

    for h in range(PARTS):
        g.vector.wait_ge(sem["mm%d" % h], 1)
        g.vector.tensor_copy(T.ys[:, lo + h * Hf:lo + (h + 1) * Hf], T["ps%d" % h][:, 0:Hf]).then_inc(sem["cp%d" % h], 1)

    for waits, trs, fold in p["calls"][core]:
        for q in waits:
            if q in tot:
                g.wait_ge(sem[q], tot[q])
        lst = []
        for d, m, rs, srcs, dst in trs:
            rid, pid = topo.addr(d, core)
            sa = [T[b][:, x0:x1] for b, x0, x1 in srcs]
            da = T[dst[0]][:, dst[1]:dst[2]]
            if fold:
                lst.append(RemoteDMATransfer(dst_ids=[DstId(rid=rid, pnc=pid)], dma_engine_mask=m, remote_sem=sem[rs],
                                             srcs=sa, dsts=[da], alu_op=1))
            else:
                lst.append(RemoteDMATransfer(dst_ids=[DstId(rid=rid, pnc=pid)], dma_engine_mask=m, remote_sem=sem[rs],
                                             src=sa[0], dst=da, alu_op=0))
        g.remote_dma_fused(lst, local_sem=sem.snt)

    nst = 0
    if isrank:
        own = [(h, -1, "cp%d" % h, (lo + h * Hf, lo + (h + 1) * Hf)) for h in range(PARTS)]
        jobs = [(q, rg) for _, _, q, rg in sorted(own + p["got"][core])]
        for q, rg in jobs:
            for a, yc, m in segs(*rg):
                dq = nextq()
                dq.wait_ge(sem[q], tot[q])
                dq.dma_start(T.y[:, yc:yc + m], T.ys[:, a:a + m]).then_inc(sem.st, 16)
                nst += 1
    g.wait_ge(sem.snt, p["sent"][core])
    if nst:
        g.wait_ge(sem.st, 16 * nst)
